import numpy as np
import ml_dtypes


def mxq(x, axis, fmt="e4m3"):
    dtype, down = {"e4m3": (ml_dtypes.float8_e4m3fn, 7), "e5m2": (ml_dtypes.float8_e5m2, 14)}[fmt]
    v = np.moveaxis(np.asarray(x, np.float32).astype(ml_dtypes.bfloat16).astype(np.float64), axis, -1)
    blocks = v.reshape(v.shape[:-1] + (-1, 32))
    amax = np.abs(blocks).max(-1, keepdims=True)
    byte = np.maximum(np.where(amax > 0, np.frexp(amax)[1] - 1 + 127, 0) - down, 1)
    scale = np.exp2(byte - 127.0)
    codes = (blocks / scale).astype(np.float32).astype(dtype).astype(np.float64)
    return np.moveaxis((codes * scale).reshape(v.shape), -1, axis)


WIDE = False


def mx_kscale(k):
    if not WIDE:
        return np.ones(k)
    levels = np.array([10, -10, 5, -5, 0])
    if k % 512:
        return np.exp2(np.random.permutation(np.resize(levels, k // 32))).repeat(32)
    a = np.empty((k // 512, 16))
    for p in range(k // 512):
        a[p, :8] = np.random.permutation(np.resize(levels, 8))
        for g in range(8):
            far = levels[np.abs(levels - a[p, g]) >= 10]
            a[p, g + 8] = far[np.random.randint(len(far))]
    return np.exp2(a.ravel()).repeat(32)


def f64(x):
    return np.asarray(x).astype(np.float64)


E2M1 = np.array([0.0, 0.5, 1.0, 1.5, 2.0, 3.0, 4.0, 6.0, -0.0, -0.5, -1.0, -1.5, -2.0, -3.0, -4.0, -6.0])


def pack_weight(w, fmt):
    k, n = w.shape
    w = f64(np.asarray(w, np.float32).astype(ml_dtypes.bfloat16)).reshape(k // 32, 32, n)
    amax = np.abs(w).max(1)
    if fmt == "e4m3":
        byte = np.frexp(amax)[1] - 1 + 127 - 7
    else:
        mant, ex = np.frexp(amax / 6.0)
        byte = np.where(mant > 0.5, ex, ex - 1) + 127
    byte = np.clip(np.where(amax > 0, byte, 1), 1, 254)
    scaled = (w * np.exp2(127.0 - byte)[:, None, :]).reshape(k, n).astype(np.float32)
    by_word = np.ascontiguousarray(scaled.reshape(k // 512, 128, 4, n).transpose(0, 1, 3, 2))
    if fmt == "e4m3":
        words = by_word.astype(ml_dtypes.float8_e4m3fn).view(np.uint8)
    else:
        c = by_word.astype(ml_dtypes.float4_e2m1fn).view(np.uint8) & 0xF
        words = (c[..., 0::2] | (c[..., 1::2] << 4)).reshape(k // 512, 128, 2 * n)
    return np.ascontiguousarray(words), np.ascontiguousarray(byte.astype(np.uint8).reshape(k // 512, 16, n))


def unpack_weight(words, scales, fmt):
    g, _, n = scales.shape
    words = np.ascontiguousarray(words).reshape(g, 128, n, -1)
    if fmt == "e4m3":
        vals = words.view(ml_dtypes.float8_e4m3fn).astype(np.float64)
    else:
        nib = np.empty((g, 128, n, 4), np.uint8)
        nib[..., 0::2] = words & 0xF
        nib[..., 1::2] = words >> 4
        vals = E2M1[nib]
    vals = vals * np.repeat(np.exp2(scales.astype(np.float64) - 127.0), 8, axis=1)[..., None]
    return vals.transpose(0, 1, 3, 2).reshape(g * 512, n)


def bf(x):
    return np.asarray(x, np.float32).astype(ml_dtypes.bfloat16)


def planes(Y):
    r, m = Y.shape
    b = f64(bf(Y)).reshape(r // 32, 32, m)
    amax = np.abs(b).max(1)
    byte = np.clip(np.where(amax > 0, np.frexp(amax)[1] - 1 + 127 - 7, 1), 1, 254)
    codes = (b * np.exp2(127.0 - byte)[:, None, :]).reshape(r, m).astype(np.float32).astype(ml_dtypes.float8_e4m3fn).view(np.uint8)
    words = codes.reshape(r // 512, 128, 4, m).transpose(0, 1, 3, 2)
    return np.ascontiguousarray(words), np.ascontiguousarray(byte.astype(np.uint8).reshape(r // 512, 16, m))


K, L, T, R, N = 1024, 512, 512, 512, 512


def setup_inputs():
    n = np.random.standard_normal
    fk = mx_kscale(K)
    fr = mx_kscale(R)
    fl = mx_kscale(L)
    xtp = pack_weight(n((K, T)) / fk[:, None], "e2m1")
    wap = pack_weight(n((K, R)) * 1 / np.sqrt(K) * fk[:, None] * fr, "e4m3")
    xqp = pack_weight(n((L, T)) / fl[:, None], "e2m1")
    wcp = pack_weight(n((L, R)) * 1 / np.sqrt(L) * fl[:, None] * fr, "e4m3")
    wbp = pack_weight(n((R, N)) * 1 / np.sqrt(R) / fr[:, None], "e2m1")
    wyp = pack_weight(n((K, N)) * 1 / np.sqrt(K) * fk[:, None], "e4m3")
    return {
        "xt_words": xtp[0],
        "xt_scales": xtp[1],
        "wa_words": wap[0],
        "wa_scales": wap[1],
        "xq_words": xqp[0],
        "xq_scales": xqp[1],
        "wc_words": wcp[0],
        "wc_scales": wcp[1],
        "wb_words": wbp[0],
        "wb_scales": wbp[1],
        "wy_words": wyp[0],
        "wy_scales": wyp[1],
    }


def reference(xt_words, xt_scales, wa_words, wa_scales, xq_words, xq_scales, wc_words, wc_scales, wb_words, wb_scales, wy_words, wy_scales):
    xtu = unpack_weight(xt_words, xt_scales, "e2m1")
    wau = unpack_weight(wa_words, wa_scales, "e4m3")
    xqu = unpack_weight(xq_words, xq_scales, "e2m1")
    wcu = unpack_weight(wc_words, wc_scales, "e4m3")
    wbu = unpack_weight(wb_words, wb_scales, "e2m1")
    wyu = unpack_weight(wy_words, wy_scales, "e4m3")
    z = wau.T @ xtu + wcu.T @ xqu
    zp = np.pad(z, ((0, 0), (1, 0)))[:, :T]
    hid = np.maximum(z, zp)
    hidq = mxq(hid, 0, "e4m3")
    y = wbu.T @ hidq + wyu.T @ xtu
    words, scales = planes(y)
    return y, words, scales

@@ -1,0 +1,200 @@
+from contextlib import ExitStack
+
+import concourse.mybir as mybir
+
+K, L, T, R, N = 1024, 512, 512, 512, 512
+FLOPS = 2 * T * (K * R + L * R + R * N + K * N)
+
+F32 = mybir.dt.float32
+BF16 = mybir.dt.bfloat16
+I32 = mybir.dt.int32
+U8 = mybir.dt.uint8
+FP8X4 = mybir.dt.float8_e4m3fn_x4
+FP4X4 = mybir.dt.float4_e2m1fn_x4
+
+P = 128
+PACK = 4
+W = 512
+CH = 128
+NCH = T // CH
+
+
+def tile_mix_hidden_peak_with_before_pl_kernel(
+    tc, xt_words, xt_scales, wa_words, wa_scales, xq_words, xq_scales, wc_words, wc_scales,
+    wb_words, wb_scales, wy_words, wy_scales, out_0, out_1, out_2,
+):
+    nc = tc.nc
+    with ExitStack() as ctx:
+        sb = ctx.enter_context(tc.tile_pool(name="sb", bufs=1))
+        ps = ctx.enter_context(tc.psum_pool(name="ps", bufs=1))
+        ctx.enter_context(tc.manual_schedule())
+
+        def sbuf(name, shape, dtype):
+            return sb.tile(shape, dtype, name=name, align_bytes=64)
+
+        order = [("xt", xt_scales), ("wa", wa_scales), ("xq", xq_scales), ("wc", wc_scales), ("wy", wy_scales), ("wb", wb_scales)]
+        first = {}
+        total = 0
+        for name, src in order:
+            first[name] = total
+            total = total + src.shape[0]
+        staged = sbuf("staged", [16, total * W], U8)
+        planes = sbuf("planes", [P, total * W], U8)
+        z_sb = sbuf("z_sb", [P, (T + 1) * PACK], F32)
+        nc.vector.memset(planes[:].bitcast(I32), 0)
+        nc.vector.memset(z_sb[:, 0:PACK], 0.0)
+
+        for i, (name, src) in enumerate(order):
+            passes = src.shape[0]
+            queue = nc.sync if i % 2 == 0 else nc.scalar
+            dst = staged[:, first[name] * W : (first[name] + passes) * W].bitcast(I32)
+            queue.dma_start(out=dst.rearrange("q (z c) -> q z c", z=passes), in_=src.bitcast(I32).rearrange("z q c -> q z c"))
+
+        def load_fp8(queue, name, src):
+            raw = sbuf(name, [P, W], I32)
+            queue.dma_start(out=raw[:], in_=src.rearrange("p c t -> p (c t)").bitcast(I32))
+            return raw
+
+        def load_fp4(queue, name, src):
+            passes = src.shape[0]
+            raw = sbuf(name, [P, passes, 2 * W], U8)
+            queue.dma_start(out=raw[:].bitcast(I32), in_=src.bitcast(I32).rearrange("z p c -> p z c"))
+            return raw
+
+        wa0_raw = load_fp8(nc.scalar, "wa0_raw", wa_words[0])
+        xt = load_fp4(nc.scalar, "xt", xt_words)
+        wa1_raw = load_fp8(nc.scalar, "wa1_raw", wa_words[1])
+        wc_raw = load_fp8(nc.scalar, "wc_raw", wc_words[0])
+        for q in range(4):
+            nc.sync.dma_start(out=planes[32 * q : 32 * q + 4, :].bitcast(I32), in_=staged[4 * q : 4 * q + 4, :].bitcast(I32))
+        xq = load_fp4(nc.sync, "xq", xq_words)
+        wy_raw = sbuf("wy_raw", [P, 2, W], I32)
+        nc.sync.dma_start(out=wy_raw[:], in_=wy_words.rearrange("z p c t -> p z (c t)").bitcast(I32))
+        wb_raw = load_fp4(nc.sync, "wb_raw", wb_words)
+
+        def plane(name, z):
+            return planes[:, (first[name] + z) * W : (first[name] + z + 1) * W]
+
+        def deal_fp8(name, raw):
+            dealt = sbuf(name, [P, W], I32)
+            nc.vector.tensor_copy(
+                out=dealt[:].rearrange("p (j c i) -> p c j i", j=PACK, i=4),
+                in_=raw.rearrange("p (c i j) -> p c j i", j=PACK, i=4),
+            )
+            return dealt
+
+        def deal_fp4(name, raw):
+            dealt = sbuf(name, [P, 2 * W], U8)
+            nc.vector.tensor_copy(
+                out=dealt[:].rearrange("p (j m b) -> p j m b", j=PACK, b=2),
+                in_=raw.rearrange("p (m j b) -> p j m b", j=PACK, b=2),
+            )
+            return dealt
+
+        def deal_scales(name, raw):
+            dealt = sbuf(name, [P, W], U8)
+            nc.vector.tensor_copy(
+                out=dealt[:].rearrange("p (j m) -> p j m", j=PACK),
+                in_=raw.rearrange("p (m j) -> p j m", j=PACK),
+            )
+            return dealt
+
+        wa0 = deal_fp8("wa0", wa0_raw[:])
+        wa0_s = deal_scales("wa0_s", plane("wa", 0))
+        wa1 = deal_fp8("wa1", wa1_raw[:])
+        wa1_s = deal_scales("wa1_s", plane("wa", 1))
+        wc = deal_fp8("wc", wc_raw[:])
+        wc_s = deal_scales("wc_s", plane("wc", 0))
+        wy0 = deal_fp8("wy0", wy_raw[:, 0, :])
+        wy0_s = deal_scales("wy0_s", plane("wy", 0))
+        wy1 = deal_fp8("wy1", wy_raw[:, 1, :])
+        wy1_s = deal_scales("wy1_s", plane("wy", 1))
+
+        def token_pass(acc, c, w, w_s, x, x_name, z, start, stop):
+            for j in range(PACK):
+                nc.tensor.matmul_mx(
+                    out=acc[:, j, :],
+                    lhsT=w[:, j * P : (j + 1) * P].bitcast(FP8X4),
+                    lhsT_scale=w_s[:, j * P : (j + 1) * P],
+                    rhs=x[:, z, 2 * c * CH : 2 * (c + 1) * CH].bitcast(FP4X4),
+                    rhs_scale=plane(x_name, z)[:, c * CH : (c + 1) * CH],
+                    start=start and j == 0,
+                    stop=stop and j == PACK - 1,
+                )
+
+        z_ps = []
+        for c in range(NCH):
+            acc = ps.tile([P, PACK, CH], F32, name="z%d" % c)
+            token_pass(acc, c, wa0, wa0_s, xt, "xt", 0, True, False)
+            token_pass(acc, c, wa1, wa1_s, xt, "xt", 1, False, False)
+            token_pass(acc, c, wc, wc_s, xq, "xq", 0, False, True)
+            lo = (c * CH + 1) * PACK
+            nc.scalar.copy(
+                out=z_sb[:, lo : lo + CH * PACK].rearrange("p (t j) -> p t j", j=PACK),
+                in_=acc[:].rearrange("p j t -> p t j"),
+            )
+            z_ps.append(acc)
+
+        def peak(c):
+            hid = sbuf("hid%d" % c, [P, CH * PACK], BF16)
+            lo = c * CH * PACK
+            nc.vector.tensor_tensor(
+                out=hid[:].rearrange("p (t j) -> p t j", j=PACK),
+                in0=z_ps[c][:].rearrange("p j t -> p t j"),
+                in1=z_sb[:, lo : lo + CH * PACK].rearrange("p (t j) -> p t j", j=PACK),
+                op=mybir.AluOpType.max,
+            )
+            return hid
+
+        def quantize_hid(c, hid):
+            codes = sbuf("hq%d" % c, [P, CH], I32)
+            scales = sbuf("hs%d" % c, [P, CH], U8)
+            nc.vector.quantize_mx(out=codes[:].bitcast(FP8X4), scales=scales[:], in_=hid[:])
+            return codes, scales
+
+        hq = []
+        hid = peak(0)
+        wb = deal_fp4("wb", wb_raw[:, 0, :])
+        hq.append(quantize_hid(0, hid))
+        hid = peak(1)
+        wb_s = deal_scales("wb_s", plane("wb", 0))
+        hq.append(quantize_hid(1, hid))
+        for c in range(2, NCH):
+            hid = peak(c)
+            hq.append(quantize_hid(c, hid))
+
+        y_codes = sbuf("y_codes", [P, T], I32)
+        y_scales = sbuf("y_scales", [P, T], U8)
+        out_rows = out_0.rearrange("(p j) t -> p j t", j=PACK)
+        out_words = out_1[0].rearrange("p c t -> p (c t)").bitcast(I32)
+        for c in range(NCH):
+            cols = slice(c * CH, (c + 1) * CH)
+            acc = ps.tile([P, PACK, CH], F32, name="y%d" % c)
+            token_pass(acc, c, wy0, wy0_s, xt, "xt", 0, True, False)
+            token_pass(acc, c, wy1, wy1_s, xt, "xt", 1, False, False)
+            codes, scales = hq[c]
+            for j in range(PACK):
+                nc.tensor.matmul_mx(
+                    out=acc[:, j, :],
+                    lhsT=wb[:, 2 * j * P : 2 * (j + 1) * P].bitcast(FP4X4),
+                    lhsT_scale=wb_s[:, j * P : (j + 1) * P],
+                    rhs=codes[:].bitcast(FP8X4),
+                    rhs_scale=scales[:],
+                    start=False,
+                    stop=j == PACK - 1,
+                )
+            y_sb = sbuf("y_sb%d" % c, [P, PACK, CH], F32)
+            nc.scalar.copy(out=y_sb[:], in_=acc[:])
+            nc.sync.dma_start(out=out_rows[:, :, cols], in_=y_sb[:])
+            y_bf = sbuf("y_bf%d" % c, [P, CH * PACK], BF16)
+            nc.vector.tensor_copy(
+                out=y_bf[:].rearrange("p (u i j) -> p u j i", i=4, j=PACK),
+                in_=y_sb[:].rearrange("p j (u i) -> p u j i", i=4),
+            )
+            nc.vector.quantize_mx(out=y_codes[:, cols].bitcast(FP8X4), scales=y_scales[:, cols], in_=y_bf[:])
+            if c == NCH - 2:
+                nc.sync.dma_start(out=out_words[:, 0 : T - CH], in_=y_codes[:, 0 : T - CH])
+        nc.sync.dma_start(out=out_words[:, T - CH : T], in_=y_codes[:, T - CH : T])
+        for q in range(4):
+            queue = nc.sync if q % 2 == 1 else nc.scalar
+            queue.dma_start(out=out_2[0, 4 * q : 4 * q + 4, :].bitcast(I32), in_=y_scales[32 * q : 32 * q + 4, :].bitcast(I32))

@@ -32,23 +32,21 @@ def tile_mix_hidden_peak_with_before_pl_kernel(
         def sbuf(name, shape, dtype):
             return sb.tile(shape, dtype, name=name, align_bytes=64)
 
-        order = [("xt", xt_scales), ("wa", wa_scales), ("xq", xq_scales), ("wc", wc_scales), ("wy", wy_scales), ("wb", wb_scales)]
-        first = {}
-        total = 0
-        for name, src in order:
-            first[name] = total
-            total = total + src.shape[0]
-        staged = sbuf("staged", [16, total * W], U8)
+        slots = {"xt": (0, 2), "wa": (1, 4), "xq": (3,), "wc": (5,), "wy": (6, 7), "wb": (8,)}
+        total = 9
+        early = 2
+        staged = sbuf("staged", [P, total, W], U8)
         planes = sbuf("planes", [P, total * W], U8)
         z_sb = sbuf("z_sb", [P, (T + 1) * PACK], F32)
         nc.vector.memset(planes[:].bitcast(I32), 0)
         nc.vector.memset(z_sb[:, 0:PACK], 0.0)
 
+        order = [("xt", xt_scales), ("wa", wa_scales), ("xq", xq_scales), ("wc", wc_scales), ("wy", wy_scales), ("wb", wb_scales)]
         for i, (name, src) in enumerate(order):
-            passes = src.shape[0]
+            lo, hi = slots[name][0], slots[name][-1]
             queue = nc.sync if i % 2 == 0 else nc.scalar
-            dst = staged[:, first[name] * W : (first[name] + passes) * W].bitcast(I32)
-            queue.dma_start(out=dst.rearrange("q (z c) -> q z c", z=passes), in_=src.bitcast(I32).rearrange("z q c -> q z c"))
+            dst = staged[:].bitcast(I32)[4:P:8, lo : hi + 1 : max(hi - lo, 1), :]
+            queue.dma_start(out=dst, in_=src.bitcast(I32).rearrange("z q c -> q z c"))
 
         def load_fp8(queue, name, src):
             raw = sbuf(name, [P, W], I32)
@@ -65,15 +63,20 @@ def tile_mix_hidden_peak_with_before_pl_kernel(
         xt = load_fp4(nc.scalar, "xt", xt_words)
         wa1_raw = load_fp8(nc.scalar, "wa1_raw", wa_words[1])
         wc_raw = load_fp8(nc.scalar, "wc_raw", wc_words[0])
-        for q in range(4):
-            nc.sync.dma_start(out=planes[32 * q : 32 * q + 4, :].bitcast(I32), in_=staged[4 * q : 4 * q + 4, :].bitcast(I32))
+        staged_words = staged[:].rearrange("p z c -> p (z c)").bitcast(I32)
+        for cols in (slice(0, early * W // 4), slice(early * W // 4, total * W // 4)):
+            for q in range(4):
+                nc.sync.dma_start(
+                    out=planes[:].bitcast(I32)[32 * q : 32 * q + 4, cols],
+                    in_=staged_words[32 * q + 4 : 32 * q + 32 : 8, cols],
+                )
         xq = load_fp4(nc.sync, "xq", xq_words)
         wy_raw = sbuf("wy_raw", [P, 2, W], I32)
         nc.sync.dma_start(out=wy_raw[:], in_=wy_words.rearrange("z p c t -> p z (c t)").bitcast(I32))
         wb_raw = load_fp4(nc.sync, "wb_raw", wb_words)
 
         def plane(name, z):
-            return planes[:, (first[name] + z) * W : (first[name] + z + 1) * W]
+            return planes[:, slots[name][z] * W : (slots[name][z] + 1) * W]
 
         def deal_fp8(name, raw):
             dealt = sbuf(name, [P, W], I32)
@@ -91,24 +94,23 @@ def tile_mix_hidden_peak_with_before_pl_kernel(
             )
             return dealt
 
-        def deal_scales(name, raw):
-            dealt = sbuf(name, [P, W], U8)
+        def deal_scales(name, first, count):
+            dealt = sbuf(name, [P, count * W], U8)
             nc.vector.tensor_copy(
-                out=dealt[:].rearrange("p (j m) -> p j m", j=PACK),
-                in_=raw.rearrange("p (m j) -> p j m", j=PACK),
+                out=dealt[:].rearrange("p (z j m) -> p z j m", z=count, j=PACK),
+                in_=planes[:, first * W : (first + count) * W].rearrange("p (z m j) -> p z j m", z=count, j=PACK),
             )
-            return dealt
+            return [dealt[:, z * W : (z + 1) * W] for z in range(count)]
 
         wa0 = deal_fp8("wa0", wa0_raw[:])
-        wa0_s = deal_scales("wa0_s", plane("wa", 0))
+        (wa0_s,) = deal_scales("wa0_s", slots["wa"][0], 1)
         wa1 = deal_fp8("wa1", wa1_raw[:])
-        wa1_s = deal_scales("wa1_s", plane("wa", 1))
         wc = deal_fp8("wc", wc_raw[:])
-        wc_s = deal_scales("wc_s", plane("wc", 0))
+        wa1_s, wc_s = deal_scales("wa1_wc_s", slots["wa"][1], 2)
+        wy0_s, wy1_s, wb_s = deal_scales("wy_wb_s", slots["wy"][0], 3)
         wy0 = deal_fp8("wy0", wy_raw[:, 0, :])
-        wy0_s = deal_scales("wy0_s", plane("wy", 0))
         wy1 = deal_fp8("wy1", wy_raw[:, 1, :])
-        wy1_s = deal_scales("wy1_s", plane("wy", 1))
+        wb = deal_fp4("wb", wb_raw[:, 0, :])
 
         def token_pass(acc, c, w, w_s, x, x_name, z, start, stop):
             for j in range(PACK):
@@ -122,10 +124,11 @@ def tile_mix_hidden_peak_with_before_pl_kernel(
                     stop=stop and j == PACK - 1,
                 )
 
-        z_ps = []
+        z_ps = [ps.tile([P, PACK, CH], F32, name="z%d" % c) for c in range(NCH)]
         for c in range(NCH):
-            acc = ps.tile([P, PACK, CH], F32, name="z%d" % c)
-            token_pass(acc, c, wa0, wa0_s, xt, "xt", 0, True, False)
+            token_pass(z_ps[c], c, wa0, wa0_s, xt, "xt", 0, True, False)
+        for c in range(NCH):
+            acc = z_ps[c]
             token_pass(acc, c, wa1, wa1_s, xt, "xt", 1, False, False)
             token_pass(acc, c, wc, wc_s, xq, "xq", 0, False, True)
             lo = (c * CH + 1) * PACK
@@ -133,7 +136,6 @@ def tile_mix_hidden_peak_with_before_pl_kernel(
                 out=z_sb[:, lo : lo + CH * PACK].rearrange("p (t j) -> p t j", j=PACK),
                 in_=acc[:].rearrange("p j t -> p t j"),
             )
-            z_ps.append(acc)
 
         def peak(c):
             hid = sbuf("hid%d" % c, [P, CH * PACK], BF16)
@@ -153,15 +155,11 @@ def tile_mix_hidden_peak_with_before_pl_kernel(
             return codes, scales
 
         hq = []
-        hid = peak(0)
-        wb = deal_fp4("wb", wb_raw[:, 0, :])
-        hq.append(quantize_hid(0, hid))
-        hid = peak(1)
-        wb_s = deal_scales("wb_s", plane("wb", 0))
-        hq.append(quantize_hid(1, hid))
-        for c in range(2, NCH):
-            hid = peak(c)
-            hq.append(quantize_hid(c, hid))
+        hid = [peak(0)]
+        for c in range(1, NCH):
+            hid.append(peak(c))
+            hq.append(quantize_hid(c - 1, hid[c - 1]))
+        hq.append(quantize_hid(NCH - 1, hid[NCH - 1]))
 
         y_codes = sbuf("y_codes", [P, T], I32)
         y_scales = sbuf("y_scales", [P, T], U8)
@@ -184,14 +182,22 @@ def tile_mix_hidden_peak_with_before_pl_kernel(
                     stop=j == PACK - 1,
                 )
             y_sb = sbuf("y_sb%d" % c, [P, PACK, CH], F32)
-            nc.scalar.copy(out=y_sb[:], in_=acc[:])
+            pieces = 2 if c == NCH - 1 else 1
+            width = CH // pieces
+            y_bf = []
+            for h in range(pieces):
+                part = slice(h * width, (h + 1) * width)
+                nc.scalar.copy(out=y_sb[:, :, part], in_=acc[:, :, part])
+                rounded = sbuf("y_bf%d_%d" % (c, h), [P, width * PACK], BF16)
+                nc.vector.tensor_copy(
+                    out=rounded[:].rearrange("p (u i j) -> p u j i", i=4, j=PACK),
+                    in_=y_sb[:, :, part].rearrange("p j (u i) -> p u j i", i=4),
+                )
+                y_bf.append(rounded)
             nc.sync.dma_start(out=out_rows[:, :, cols], in_=y_sb[:])
-            y_bf = sbuf("y_bf%d" % c, [P, CH * PACK], BF16)
-            nc.vector.tensor_copy(
-                out=y_bf[:].rearrange("p (u i j) -> p u j i", i=4, j=PACK),
-                in_=y_sb[:].rearrange("p j (u i) -> p u j i", i=4),
-            )
-            nc.vector.quantize_mx(out=y_codes[:, cols].bitcast(FP8X4), scales=y_scales[:, cols], in_=y_bf[:])
+            for h in range(pieces):
+                part = slice(c * CH + h * width, c * CH + (h + 1) * width)
+                nc.vector.quantize_mx(out=y_codes[:, part].bitcast(FP8X4), scales=y_scales[:, part], in_=y_bf[h][:])
             if c == NCH - 2:
                 nc.sync.dma_start(out=out_words[:, 0 : T - CH], in_=y_codes[:, 0 : T - CH])
         nc.sync.dma_start(out=out_words[:, T - CH : T], in_=y_codes[:, T - CH : T])

@@ -32,21 +32,29 @@ def tile_mix_hidden_peak_with_before_pl_kernel(
         def sbuf(name, shape, dtype):
             return sb.tile(shape, dtype, name=name, align_bytes=64)
 
-        slots = {"xt": (0, 2), "wa": (1, 4), "xq": (3,), "wc": (5,), "wy": (6, 7), "wb": (8,)}
-        total = 9
-        early = 2
-        staged = sbuf("staged", [P, total, W], U8)
-        planes = sbuf("planes", [P, total * W], U8)
+        slots = {"xt": (0, 3), "wa": (1, 4), "xq": (2,), "wc": (5,), "wb": (6,), "wy": (7, 8)}
+        staged = sbuf("staged", [P, 3 * W], U8)
+        parked = sbuf("parked", [P, 5 * W], U8)
+        planes = sbuf("planes", [P, 9 * W], U8)
         z_sb = sbuf("z_sb", [P, (T + 1) * PACK], F32)
+        nc.vector.memset(staged[:, 0:W].bitcast(I32), 0)
+        nc.vector.memset(staged[:, W : 3 * W].bitcast(I32), 0)
         nc.vector.memset(planes[:].bitcast(I32), 0)
         nc.vector.memset(z_sb[:, 0:PACK], 0.0)
 
-        order = [("xt", xt_scales), ("wa", wa_scales), ("xq", xq_scales), ("wc", wc_scales), ("wy", wy_scales), ("wb", wb_scales)]
-        for i, (name, src) in enumerate(order):
-            lo, hi = slots[name][0], slots[name][-1]
-            queue = nc.sync if i % 2 == 0 else nc.scalar
-            dst = staged[:].bitcast(I32)[4:P:8, lo : hi + 1 : max(hi - lo, 1), :]
-            queue.dma_start(out=dst, in_=src.bitcast(I32).rearrange("z q c -> q z c"))
+        def words(tile, rows, first, count):
+            return tile[:].bitcast(I32)[rows, first * W // 4 : (first + count) * W // 4]
+
+        both, upper, third = slice(0, P, 4), slice(64, P, 4), slice(1, 64, 4)
+        nc.sync.dma_start(out=words(parked, both, 1, 1), in_=xt_scales.bitcast(I32).rearrange("z q c -> (z q) c"))
+        nc.scalar.dma_start(out=words(parked, upper, 0, 1), in_=xq_scales[0].bitcast(I32))
+        nc.sync.dma_start(out=words(staged, both, 0, 1), in_=wa_scales.bitcast(I32).rearrange("z q c -> (z q) c"))
+        nc.scalar.dma_start(out=words(staged, third, 0, 1), in_=wb_scales[0].bitcast(I32))
+        nc.sync.dma_start(out=words(staged, upper, 1, 1), in_=wc_scales[0].bitcast(I32))
+        nc.scalar.dma_start(
+            out=words(staged, third, 1, 2).rearrange("q (z c) -> q z c", z=2),
+            in_=wy_scales.bitcast(I32).rearrange("z q c -> q z c"),
+        )
 
         def load_fp8(queue, name, src):
             raw = sbuf(name, [P, W], I32)
@@ -54,26 +62,37 @@ def tile_mix_hidden_peak_with_before_pl_kernel(
             return raw
 
         def load_fp4(queue, name, src):
-            passes = src.shape[0]
-            raw = sbuf(name, [P, passes, 2 * W], U8)
-            queue.dma_start(out=raw[:].bitcast(I32), in_=src.bitcast(I32).rearrange("z p c -> p z c"))
+            raw = sbuf(name, [P, 2 * W], U8)
+            queue.dma_start(out=raw[:].bitcast(I32), in_=src.bitcast(I32))
             return raw
 
-        wa0_raw = load_fp8(nc.scalar, "wa0_raw", wa_words[0])
-        xt = load_fp4(nc.scalar, "xt", xt_words)
-        wa1_raw = load_fp8(nc.scalar, "wa1_raw", wa_words[1])
-        wc_raw = load_fp8(nc.scalar, "wc_raw", wc_words[0])
-        staged_words = staged[:].rearrange("p z c -> p (z c)").bitcast(I32)
-        for cols in (slice(0, early * W // 4), slice(early * W // 4, total * W // 4)):
-            for q in range(4):
-                nc.sync.dma_start(
-                    out=planes[:].bitcast(I32)[32 * q : 32 * q + 4, cols],
-                    in_=staged_words[32 * q + 4 : 32 * q + 32 : 8, cols],
+        def deal_scales(first, count):
+            nc.vector.tensor_copy(
+                out=parked[:, (2 + first) * W : (2 + first + count) * W].rearrange("p (z j m) -> p z j m", z=count, j=PACK),
+                in_=staged[:, first * W : (first + count) * W].rearrange("p (z m j) -> p z j m", z=count, j=PACK),
+            )
+
+        def move_scales(queues, base, first, count, slot):
+            for r in range(4):
+                queues[r % len(queues)].dma_start(
+                    out=words(planes, slice(r, P, 32), slot, count),
+                    in_=words(parked, slice(base + 4 * r, base + 4 * r + 49, 16), first, count),
                 )
-        xq = load_fp4(nc.sync, "xq", xq_words)
+
+        wa0_raw = load_fp8(nc.scalar, "wa0_raw", wa_words[0])
+        xt_raw = sbuf("xt_raw", [P, 2, 2 * W], U8)
+        nc.scalar.dma_start(out=xt_raw[:].bitcast(I32), in_=xt_words.bitcast(I32).rearrange("z p c -> p z c"))
+        deal_scales(0, 1)
+        deal_scales(1, 2)
+        move_scales([nc.sync, nc.scalar], 0, 1, 2, 0)
+        move_scales([nc.sync], 64, 0, 4, 2)
+        wa1_raw = load_fp8(nc.sync, "wa1_raw", wa_words[1])
+        wc_raw = load_fp8(nc.sync, "wc_raw", wc_words[0])
+        xq = load_fp4(nc.sync, "xq", xq_words[0])
+        wb_raw = load_fp4(nc.sync, "wb_raw", wb_words[0])
         wy_raw = sbuf("wy_raw", [P, 2, W], I32)
         nc.sync.dma_start(out=wy_raw[:], in_=wy_words.rearrange("z p c t -> p z (c t)").bitcast(I32))
-        wb_raw = load_fp4(nc.sync, "wb_raw", wb_words)
+        move_scales([nc.sync], 1, 2, 3, 6)
 
         def plane(name, z):
             return planes[:, slots[name][z] * W : (slots[name][z] + 1) * W]
@@ -94,23 +113,15 @@ def tile_mix_hidden_peak_with_before_pl_kernel(
             )
             return dealt
 
-        def deal_scales(name, first, count):
-            dealt = sbuf(name, [P, count * W], U8)
-            nc.vector.tensor_copy(
-                out=dealt[:].rearrange("p (z j m) -> p z j m", z=count, j=PACK),
-                in_=planes[:, first * W : (first + count) * W].rearrange("p (z m j) -> p z j m", z=count, j=PACK),
-            )
-            return [dealt[:, z * W : (z + 1) * W] for z in range(count)]
-
         wa0 = deal_fp8("wa0", wa0_raw[:])
-        (wa0_s,) = deal_scales("wa0_s", slots["wa"][0], 1)
         wa1 = deal_fp8("wa1", wa1_raw[:])
         wc = deal_fp8("wc", wc_raw[:])
-        wa1_s, wc_s = deal_scales("wa1_wc_s", slots["wa"][1], 2)
-        wy0_s, wy1_s, wb_s = deal_scales("wy_wb_s", slots["wy"][0], 3)
+        wb = deal_fp4("wb", wb_raw[:])
         wy0 = deal_fp8("wy0", wy_raw[:, 0, :])
         wy1 = deal_fp8("wy1", wy_raw[:, 1, :])
-        wb = deal_fp4("wb", wb_raw[:, 0, :])
+        wa0_s, wa1_s, wc_s = plane("wa", 0), plane("wa", 1), plane("wc", 0)
+        wy0_s, wy1_s, wb_s = plane("wy", 0), plane("wy", 1), plane("wb", 0)
+        xt = [xt_raw[:, 0, :], xt_raw[:, 1, :]]
 
         def token_pass(acc, c, w, w_s, x, x_name, z, start, stop):
             for j in range(PACK):
@@ -118,7 +129,7 @@ def tile_mix_hidden_peak_with_before_pl_kernel(
                     out=acc[:, j, :],
                     lhsT=w[:, j * P : (j + 1) * P].bitcast(FP8X4),
                     lhsT_scale=w_s[:, j * P : (j + 1) * P],
-                    rhs=x[:, z, 2 * c * CH : 2 * (c + 1) * CH].bitcast(FP4X4),
+                    rhs=x[z][:, 2 * c * CH : 2 * (c + 1) * CH].bitcast(FP4X4),
                     rhs_scale=plane(x_name, z)[:, c * CH : (c + 1) * CH],
                     start=start and j == 0,
                     stop=stop and j == PACK - 1,
@@ -130,7 +141,7 @@ def tile_mix_hidden_peak_with_before_pl_kernel(
         for c in range(NCH):
             acc = z_ps[c]
             token_pass(acc, c, wa1, wa1_s, xt, "xt", 1, False, False)
-            token_pass(acc, c, wc, wc_s, xq, "xq", 0, False, True)
+            token_pass(acc, c, wc, wc_s, [xq[:]], "xq", 0, False, True)
             lo = (c * CH + 1) * PACK
             nc.scalar.copy(
                 out=z_sb[:, lo : lo + CH * PACK].rearrange("p (t j) -> p t j", j=PACK),

@@ -17,6 +17,7 @@ PACK = 4
 W = 512
 CH = 128
 NCH = T // CH
+RUN = 4
 
 
 def tile_mix_hidden_peak_with_before_pl_kernel(
@@ -32,76 +33,75 @@ def tile_mix_hidden_peak_with_before_pl_kernel(
         def sbuf(name, shape, dtype):
             return sb.tile(shape, dtype, name=name, align_bytes=64)
 
-        slots = {"xt": (0, 3), "wa": (1, 4), "xq": (2,), "wc": (5,), "wb": (6,), "wy": (7, 8)}
-        staged = sbuf("staged", [P, 3 * W], U8)
-        parked = sbuf("parked", [P, 5 * W], U8)
-        planes = sbuf("planes", [P, 9 * W], U8)
-        z_sb = sbuf("z_sb", [P, (T + 1) * PACK], F32)
-        nc.vector.memset(staged[:, 0:W].bitcast(I32), 0)
-        nc.vector.memset(staged[:, W : 3 * W].bitcast(I32), 0)
-        nc.vector.memset(planes[:].bitcast(I32), 0)
-        nc.vector.memset(z_sb[:, 0:PACK], 0.0)
-
-        def words(tile, rows, first, count):
+        def spans(tile, rows, first, count):
             return tile[:].bitcast(I32)[rows, first * W // 4 : (first + count) * W // 4]
 
-        both, upper, third = slice(0, P, 4), slice(64, P, 4), slice(1, 64, 4)
-        nc.sync.dma_start(out=words(parked, both, 1, 1), in_=xt_scales.bitcast(I32).rearrange("z q c -> (z q) c"))
-        nc.scalar.dma_start(out=words(parked, upper, 0, 1), in_=xq_scales[0].bitcast(I32))
-        nc.sync.dma_start(out=words(staged, both, 0, 1), in_=wa_scales.bitcast(I32).rearrange("z q c -> (z q) c"))
-        nc.scalar.dma_start(out=words(staged, third, 0, 1), in_=wb_scales[0].bitcast(I32))
-        nc.sync.dma_start(out=words(staged, upper, 1, 1), in_=wc_scales[0].bitcast(I32))
-        nc.scalar.dma_start(
-            out=words(staged, third, 1, 2).rearrange("q (z c) -> q z c", z=2),
+        staged = sbuf("staged", [P, 3 * W], U8)
+        staged_dealt = sbuf("staged_dealt", [P, 3 * W], U8)
+        parked = sbuf("parked", [P, 4 * W], U8)
+        planes_first = sbuf("planes_first", [P, 2 * W], U8)
+        planes_rest = sbuf("planes_rest", [P, 4 * W], U8)
+        planes_second = sbuf("planes_second", [P, 3 * W], U8)
+        z_sb = sbuf("z_sb", [P, (T + 1) * PACK], F32)
+        nc.vector.memset(staged[:].bitcast(I32), 0)
+        for planes in (planes_first, planes_rest, planes_second):
+            nc.vector.memset(planes[:].bitcast(I32), 0)
+        nc.vector.memset(z_sb[:, 0:PACK], 0.0)
+
+        bases_0_and_64, base_64, base_1 = slice(0, P, 4), slice(64, P, 4), slice(1, 64, 4)
+        nc.sync.dma_start(out=spans(parked, bases_0_and_64, 2, 1), in_=wa_scales.bitcast(I32).rearrange("z q c -> (z q) c"))
+        nc.scalar.dma_start(out=spans(parked, bases_0_and_64, 1, 1), in_=xt_scales.bitcast(I32).rearrange("z q c -> (z q) c"))
+        nc.sync.dma_start(out=spans(parked, base_64, 3, 1), in_=wc_scales[0].bitcast(I32))
+        nc.scalar.dma_start(out=spans(parked, base_64, 0, 1), in_=xq_scales[0].bitcast(I32))
+        nc.sync.dma_start(
+            out=spans(staged, base_1, 1, 2).rearrange("q (z c) -> q z c", z=2),
             in_=wy_scales.bitcast(I32).rearrange("z q c -> q z c"),
         )
+        nc.sync.dma_start(out=spans(staged, base_1, 0, 1), in_=wb_scales[0].bitcast(I32))
+
+        def deal_scales(dealt, raw, passes, j_lo, j_hi):
+            nc.vector.tensor_copy(
+                out=dealt.rearrange("p (z j m) -> p z j m", z=passes, j=PACK)[:, :, j_lo:j_hi, :],
+                in_=raw.rearrange("p (z m j) -> p z j m", z=passes, j=PACK)[:, :, j_lo:j_hi, :],
+            )
+
+        def move_scales(planes, source, base, first, count):
+            for r in range(4):
+                nc.sync.dma_start(
+                    out=spans(planes, slice(r, P, 32), 0, count),
+                    in_=spans(source, slice(base + 4 * r, base + 64, 16), first, count),
+                )
+
+        def plane(planes, place):
+            return planes[:, place * W : (place + 1) * W]
 
         def load_fp8(queue, name, src):
-            raw = sbuf(name, [P, W], I32)
-            queue.dma_start(out=raw[:], in_=src.rearrange("p c t -> p (c t)").bitcast(I32))
+            raw = sbuf(name, [P, src.shape[0], W], I32)
+            queue.dma_start(out=raw[:], in_=src.rearrange("z p c t -> p z (c t)").bitcast(I32))
             return raw
 
         def load_fp4(queue, name, src):
-            raw = sbuf(name, [P, 2 * W], U8)
-            queue.dma_start(out=raw[:].bitcast(I32), in_=src.bitcast(I32))
+            raw = sbuf(name, [P, src.shape[0], 2 * W], U8)
+            queue.dma_start(out=raw[:].bitcast(I32), in_=src.bitcast(I32).rearrange("z p c -> p z c"))
             return raw
 
-        def deal_scales(first, count):
-            nc.vector.tensor_copy(
-                out=parked[:, (2 + first) * W : (2 + first + count) * W].rearrange("p (z j m) -> p z j m", z=count, j=PACK),
-                in_=staged[:, first * W : (first + count) * W].rearrange("p (z m j) -> p z j m", z=count, j=PACK),
-            )
-
-        def move_scales(queues, base, first, count, slot):
-            for r in range(4):
-                queues[r % len(queues)].dma_start(
-                    out=words(planes, slice(r, P, 32), slot, count),
-                    in_=words(parked, slice(base + 4 * r, base + 4 * r + 49, 16), first, count),
-                )
-
-        wa0_raw = load_fp8(nc.scalar, "wa0_raw", wa_words[0])
-        xt_raw = sbuf("xt_raw", [P, 2, 2 * W], U8)
-        nc.scalar.dma_start(out=xt_raw[:].bitcast(I32), in_=xt_words.bitcast(I32).rearrange("z p c -> p z c"))
-        deal_scales(0, 1)
-        deal_scales(1, 2)
-        move_scales([nc.sync, nc.scalar], 0, 1, 2, 0)
-        move_scales([nc.sync], 64, 0, 4, 2)
-        wa1_raw = load_fp8(nc.sync, "wa1_raw", wa_words[1])
-        wc_raw = load_fp8(nc.sync, "wc_raw", wc_words[0])
-        xq = load_fp4(nc.sync, "xq", xq_words[0])
-        wb_raw = load_fp4(nc.sync, "wb_raw", wb_words[0])
-        wy_raw = sbuf("wy_raw", [P, 2, W], I32)
-        nc.sync.dma_start(out=wy_raw[:], in_=wy_words.rearrange("z p c t -> p z (c t)").bitcast(I32))
-        move_scales([nc.sync], 1, 2, 3, 6)
-
-        def plane(name, z):
-            return planes[:, slots[name][z] * W : (slots[name][z] + 1) * W]
+        wa_raw = load_fp8(nc.scalar, "wa_raw", wa_words)
+        xt = load_fp4(nc.scalar, "xt", xt_words)
+        deal_scales(staged_dealt[:, W : 3 * W], staged[:, W : 3 * W], 2, 0, PACK)
+        move_scales(planes_first, parked, 0, 1, 2)
+        move_scales(planes_rest, parked, 64, 0, 4)
+        wc_raw = load_fp8(nc.sync, "wc_raw", wc_words)
+        xq = load_fp4(nc.sync, "xq", xq_words)
+        wb_raw = load_fp4(nc.sync, "wb_raw", wb_words)
+        wy_raw = load_fp8(nc.sync, "wy_raw", wy_words)
+        xt0_plane, xq_plane, xt1_plane = plane(planes_first, 0), plane(planes_rest, 0), plane(planes_rest, 1)
+        wb_plane, wy0_plane, wy1_plane = (plane(planes_second, place) for place in range(3))
 
         def deal_fp8(name, raw):
             dealt = sbuf(name, [P, W], I32)
             nc.vector.tensor_copy(
-                out=dealt[:].rearrange("p (j c i) -> p c j i", j=PACK, i=4),
-                in_=raw.rearrange("p (c i j) -> p c j i", j=PACK, i=4),
+                out=dealt[:].rearrange("p (j c i) -> p c j i", j=PACK, i=RUN),
+                in_=raw.rearrange("p (c i j) -> p c j i", j=PACK, i=RUN),
             )
             return dealt
 
@@ -113,39 +113,46 @@ def tile_mix_hidden_peak_with_before_pl_kernel(
             )
             return dealt
 
-        wa0 = deal_fp8("wa0", wa0_raw[:])
-        wa1 = deal_fp8("wa1", wa1_raw[:])
-        wc = deal_fp8("wc", wc_raw[:])
-        wb = deal_fp4("wb", wb_raw[:])
+        wa0_scales = sbuf("wa0_scales", [P, W], U8)
+        wa1_wc_scales = sbuf("wa1_wc_scales", [P, 2 * W], U8)
+        wa0 = deal_fp8("wa0", wa_raw[:, 0, :])
+        deal_scales(wa0_scales[:], plane(planes_first, 1), 1, 0, 1)
+        deal_scales(wa0_scales[:], plane(planes_first, 1), 1, 1, PACK)
+        wa1 = deal_fp8("wa1", wa_raw[:, 1, :])
+        deal_scales(staged_dealt[:, 0:W], staged[:, 0:W], 1, 0, PACK)
+        move_scales(planes_second, staged_dealt, 1, 0, 3)
+        deal_scales(wa1_wc_scales[:], planes_rest[:, 2 * W : 4 * W], 2, 0, PACK)
+        wc = deal_fp8("wc", wc_raw[:, 0, :])
+        wb = deal_fp4("wb", wb_raw[:, 0, :])
         wy0 = deal_fp8("wy0", wy_raw[:, 0, :])
         wy1 = deal_fp8("wy1", wy_raw[:, 1, :])
-        wa0_s, wa1_s, wc_s = plane("wa", 0), plane("wa", 1), plane("wc", 0)
-        wy0_s, wy1_s, wb_s = plane("wy", 0), plane("wy", 1), plane("wb", 0)
-        xt = [xt_raw[:, 0, :], xt_raw[:, 1, :]]
 
-        def token_pass(acc, c, w, w_s, x, x_name, z, start, stop):
+        def token_matmul(acc, c, j, weight, weight_scales, tokens, token_scales, start, stop):
+            nc.tensor.matmul_mx(
+                out=acc[:, j, :],
+                lhsT=weight[:, j * P : (j + 1) * P].bitcast(FP8X4),
+                lhsT_scale=weight_scales[:, j * P : (j + 1) * P],
+                rhs=tokens[:, 2 * c * CH : 2 * (c + 1) * CH].bitcast(FP4X4),
+                rhs_scale=token_scales[:, c * CH : (c + 1) * CH],
+                start=start,
+                stop=stop,
+            )
+
+        def token_pass(acc, c, weight, weight_scales, tokens, token_scales, start, stop):
             for j in range(PACK):
-                nc.tensor.matmul_mx(
-                    out=acc[:, j, :],
-                    lhsT=w[:, j * P : (j + 1) * P].bitcast(FP8X4),
-                    lhsT_scale=w_s[:, j * P : (j + 1) * P],
-                    rhs=x[z][:, 2 * c * CH : 2 * (c + 1) * CH].bitcast(FP4X4),
-                    rhs_scale=plane(x_name, z)[:, c * CH : (c + 1) * CH],
-                    start=start and j == 0,
-                    stop=stop and j == PACK - 1,
-                )
+                token_matmul(acc, c, j, weight, weight_scales, tokens, token_scales, start and j == 0, stop and j == PACK - 1)
 
         z_ps = [ps.tile([P, PACK, CH], F32, name="z%d" % c) for c in range(NCH)]
+        for j in range(PACK):
+            for c in range(NCH):
+                token_matmul(z_ps[c], c, j, wa0, wa0_scales[:], xt[:, 0, :], xt0_plane, j == 0, False)
         for c in range(NCH):
-            token_pass(z_ps[c], c, wa0, wa0_s, xt, "xt", 0, True, False)
-        for c in range(NCH):
-            acc = z_ps[c]
-            token_pass(acc, c, wa1, wa1_s, xt, "xt", 1, False, False)
-            token_pass(acc, c, wc, wc_s, [xq[:]], "xq", 0, False, True)
+            token_pass(z_ps[c], c, wa1, wa1_wc_scales[:, 0:W], xt[:, 1, :], xt1_plane, False, False)
+            token_pass(z_ps[c], c, wc, wa1_wc_scales[:, W : 2 * W], xq[:, 0, :], xq_plane, False, True)
             lo = (c * CH + 1) * PACK
             nc.scalar.copy(
                 out=z_sb[:, lo : lo + CH * PACK].rearrange("p (t j) -> p t j", j=PACK),
-                in_=acc[:].rearrange("p j t -> p t j"),
+                in_=z_ps[c][:].rearrange("p j t -> p t j"),
             )
 
         def peak(c):
@@ -160,58 +167,81 @@ def tile_mix_hidden_peak_with_before_pl_kernel(
             return hid
 
         def quantize_hid(c, hid):
-            codes = sbuf("hq%d" % c, [P, CH], I32)
-            scales = sbuf("hs%d" % c, [P, CH], U8)
+            codes = sbuf("hid_codes%d" % c, [P, CH], I32)
+            scales = sbuf("hid_scales%d" % c, [P, CH], U8)
             nc.vector.quantize_mx(out=codes[:].bitcast(FP8X4), scales=scales[:], in_=hid[:])
             return codes, scales
-
-        hq = []
-        hid = [peak(0)]
-        for c in range(1, NCH):
-            hid.append(peak(c))
-            hq.append(quantize_hid(c - 1, hid[c - 1]))
-        hq.append(quantize_hid(NCH - 1, hid[NCH - 1]))
 
         y_codes = sbuf("y_codes", [P, T], I32)
         y_scales = sbuf("y_scales", [P, T], U8)
         out_rows = out_0.rearrange("(p j) t -> p j t", j=PACK)
         out_words = out_1[0].rearrange("p c t -> p (c t)").bitcast(I32)
-        for c in range(NCH):
-            cols = slice(c * CH, (c + 1) * CH)
+
+        def second_layer(c, codes, scales):
             acc = ps.tile([P, PACK, CH], F32, name="y%d" % c)
-            token_pass(acc, c, wy0, wy0_s, xt, "xt", 0, True, False)
-            token_pass(acc, c, wy1, wy1_s, xt, "xt", 1, False, False)
-            codes, scales = hq[c]
+            token_pass(acc, c, wy0, wy0_plane, xt[:, 0, :], xt0_plane, True, False)
+            token_pass(acc, c, wy1, wy1_plane, xt[:, 1, :], xt1_plane, False, False)
             for j in range(PACK):
                 nc.tensor.matmul_mx(
                     out=acc[:, j, :],
                     lhsT=wb[:, 2 * j * P : 2 * (j + 1) * P].bitcast(FP4X4),
-                    lhsT_scale=wb_s[:, j * P : (j + 1) * P],
+                    lhsT_scale=wb_plane[:, j * P : (j + 1) * P],
                     rhs=codes[:].bitcast(FP8X4),
                     rhs_scale=scales[:],
                     start=False,
                     stop=j == PACK - 1,
                 )
             y_sb = sbuf("y_sb%d" % c, [P, PACK, CH], F32)
-            pieces = 2 if c == NCH - 1 else 1
-            width = CH // pieces
-            y_bf = []
-            for h in range(pieces):
-                part = slice(h * width, (h + 1) * width)
-                nc.scalar.copy(out=y_sb[:, :, part], in_=acc[:, :, part])
-                rounded = sbuf("y_bf%d_%d" % (c, h), [P, width * PACK], BF16)
-                nc.vector.tensor_copy(
-                    out=rounded[:].rearrange("p (u i j) -> p u j i", i=4, j=PACK),
-                    in_=y_sb[:, :, part].rearrange("p j (u i) -> p u j i", i=4),
-                )
-                y_bf.append(rounded)
-            nc.sync.dma_start(out=out_rows[:, :, cols], in_=y_sb[:])
-            for h in range(pieces):
-                part = slice(c * CH + h * width, c * CH + (h + 1) * width)
-                nc.vector.quantize_mx(out=y_codes[:, part].bitcast(FP8X4), scales=y_scales[:, part], in_=y_bf[h][:])
-            if c == NCH - 2:
-                nc.sync.dma_start(out=out_words[:, 0 : T - CH], in_=y_codes[:, 0 : T - CH])
-        nc.sync.dma_start(out=out_words[:, T - CH : T], in_=y_codes[:, T - CH : T])
-        for q in range(4):
-            queue = nc.sync if q % 2 == 1 else nc.scalar
-            queue.dma_start(out=out_2[0, 4 * q : 4 * q + 4, :].bitcast(I32), in_=y_scales[32 * q : 32 * q + 4, :].bitcast(I32))
+            return acc, y_sb
+
+        def copy_and_round(acc, y_sb, name, lo, hi):
+            nc.scalar.copy(out=y_sb[:, :, lo:hi], in_=acc[:, :, lo:hi])
+            rounded = sbuf(name, [P, (hi - lo) * PACK], BF16)
+            nc.vector.tensor_copy(
+                out=rounded[:].rearrange("p (u i j) -> p u j i", i=RUN, j=PACK),
+                in_=y_sb[:, :, lo:hi].rearrange("p j (u i) -> p u j i", i=RUN),
+            )
+            return rounded
+
+        def quantize_y(rounded, lo, hi):
+            nc.vector.quantize_mx(out=y_codes[:, lo:hi].bitcast(FP8X4), scales=y_scales[:, lo:hi], in_=rounded[:])
+
+        def store_y(c, y_sb):
+            nc.sync.dma_start(out=out_rows[:, :, c * CH : (c + 1) * CH], in_=y_sb[:])
+
+        def store_codes(lo, hi):
+            nc.sync.dma_start(out=out_words[:, lo:hi], in_=y_codes[:, lo:hi])
+
+        last = NCH - 1
+        hid = [peak(0)]
+        hid_mx = []
+        for c in range(1, NCH):
+            hid.append(peak(c))
+            hid_mx.append(quantize_hid(c - 1, hid[c - 1]))
+
+        rounded = []
+        for c in range(last):
+            acc, y_sb = second_layer(c, *hid_mx[c])
+            rounded.append(copy_and_round(acc, y_sb, "y_bf%d" % c, 0, CH))
+            store_y(c, y_sb)
+            if c == 0:
+                hid_mx.append(quantize_hid(last, hid[last]))
+            else:
+                quantize_y(rounded[c - 1], (c - 1) * CH, c * CH)
+        store_codes(0, (last - 1) * CH)
+
+        half = CH // 2
+        acc, y_sb = second_layer(last, *hid_mx[last])
+        first_half = copy_and_round(acc, y_sb, "y_bf_first_half", 0, half)
+        quantize_y(rounded[last - 1], (last - 1) * CH, last * CH)
+        second_half = copy_and_round(acc, y_sb, "y_bf_second_half", half, CH)
+        store_y(last, y_sb)
+        quantize_y(first_half, last * CH, last * CH + half)
+        quantize_y(second_half, last * CH + half, T)
+        store_codes((last - 1) * CH, T)
+        for quad in range(4):
+            queue = nc.sync if quad % 2 == 1 else nc.scalar
+            queue.dma_start(
+                out=out_2[0, 4 * quad : 4 * quad + 4, :].bitcast(I32),
+                in_=y_scales[32 * quad : 32 * quad + 4, :].bitcast(I32),
+            )

from contextlib import ExitStack

import concourse.mybir as mybir

K, L, T, R, N = 1024, 512, 512, 512, 512
FLOPS = 2 * T * (K * R + L * R + R * N + K * N)

F32 = mybir.dt.float32
BF16 = mybir.dt.bfloat16
I32 = mybir.dt.int32
U8 = mybir.dt.uint8
FP8X4 = mybir.dt.float8_e4m3fn_x4
FP4X4 = mybir.dt.float4_e2m1fn_x4

P = 128
PACK = 4
W = 512
CH = 128
NCH = T // CH
RUN = 4


def tile_mix_hidden_peak_with_before_pl_kernel(
    tc, xt_words, xt_scales, wa_words, wa_scales, xq_words, xq_scales, wc_words, wc_scales,
    wb_words, wb_scales, wy_words, wy_scales, out_0, out_1, out_2,
):
    nc = tc.nc
    with ExitStack() as ctx:
        sb = ctx.enter_context(tc.tile_pool(name="sb", bufs=1))
        ps = ctx.enter_context(tc.psum_pool(name="ps", bufs=1))
        ctx.enter_context(tc.manual_schedule())

        def sbuf(name, shape, dtype):
            return sb.tile(shape, dtype, name=name, align_bytes=64)

        def spans(tile, rows, first, count):
            return tile[:].bitcast(I32)[rows, first * W // 4 : (first + count) * W // 4]

        staged = sbuf("staged", [P, 3 * W], U8)
        staged_dealt = sbuf("staged_dealt", [P, 3 * W], U8)
        parked = sbuf("parked", [P, 4 * W], U8)
        planes_first = sbuf("planes_first", [P, 2 * W], U8)
        planes_rest = sbuf("planes_rest", [P, 4 * W], U8)
        planes_second = sbuf("planes_second", [P, 3 * W], U8)
        z_sb = sbuf("z_sb", [P, (T + 1) * PACK], F32)
        nc.vector.memset(staged[:].bitcast(I32), 0)
        for planes in (planes_first, planes_rest, planes_second):
            nc.vector.memset(planes[:].bitcast(I32), 0)
        nc.vector.memset(z_sb[:, 0:PACK], 0.0)

        bases_0_and_64, base_64, base_1 = slice(0, P, 4), slice(64, P, 4), slice(1, 64, 4)
        nc.sync.dma_start(out=spans(parked, bases_0_and_64, 2, 1), in_=wa_scales.bitcast(I32).rearrange("z q c -> (z q) c"))
        nc.scalar.dma_start(out=spans(parked, bases_0_and_64, 1, 1), in_=xt_scales.bitcast(I32).rearrange("z q c -> (z q) c"))
        nc.sync.dma_start(out=spans(parked, base_64, 3, 1), in_=wc_scales[0].bitcast(I32))
        nc.scalar.dma_start(out=spans(parked, base_64, 0, 1), in_=xq_scales[0].bitcast(I32))
        nc.sync.dma_start(
            out=spans(staged, base_1, 1, 2).rearrange("q (z c) -> q z c", z=2),
            in_=wy_scales.bitcast(I32).rearrange("z q c -> q z c"),
        )
        nc.sync.dma_start(out=spans(staged, base_1, 0, 1), in_=wb_scales[0].bitcast(I32))

        def deal_scales(dealt, raw, passes, j_lo, j_hi):
            nc.vector.tensor_copy(
                out=dealt.rearrange("p (z j m) -> p z j m", z=passes, j=PACK)[:, :, j_lo:j_hi, :],
                in_=raw.rearrange("p (z m j) -> p z j m", z=passes, j=PACK)[:, :, j_lo:j_hi, :],
            )

        def move_scales(planes, source, base, first, count):
            for r in range(4):
                nc.sync.dma_start(
                    out=spans(planes, slice(r, P, 32), 0, count),
                    in_=spans(source, slice(base + 4 * r, base + 64, 16), first, count),
                )

        def plane(planes, place):
            return planes[:, place * W : (place + 1) * W]

        def load_fp8(queue, name, src):
            raw = sbuf(name, [P, src.shape[0], W], I32)
            queue.dma_start(out=raw[:], in_=src.rearrange("z p c t -> p z (c t)").bitcast(I32))
            return raw

        def load_fp4(queue, name, src):
            raw = sbuf(name, [P, src.shape[0], 2 * W], U8)
            queue.dma_start(out=raw[:].bitcast(I32), in_=src.bitcast(I32).rearrange("z p c -> p z c"))
            return raw

        wa_raw = load_fp8(nc.scalar, "wa_raw", wa_words)
        xt = load_fp4(nc.scalar, "xt", xt_words)
        deal_scales(staged_dealt[:, W : 3 * W], staged[:, W : 3 * W], 2, 0, PACK)
        move_scales(planes_first, parked, 0, 1, 2)
        move_scales(planes_rest, parked, 64, 0, 4)
        wc_raw = load_fp8(nc.sync, "wc_raw", wc_words)
        xq = load_fp4(nc.sync, "xq", xq_words)
        wb_raw = load_fp4(nc.sync, "wb_raw", wb_words)
        wy_raw = load_fp8(nc.sync, "wy_raw", wy_words)
        xt0_plane, xq_plane, xt1_plane = plane(planes_first, 0), plane(planes_rest, 0), plane(planes_rest, 1)
        wb_plane, wy0_plane, wy1_plane = (plane(planes_second, place) for place in range(3))

        def deal_fp8(name, raw):
            dealt = sbuf(name, [P, W], I32)
            nc.vector.tensor_copy(
                out=dealt[:].rearrange("p (j c i) -> p c j i", j=PACK, i=RUN),
                in_=raw.rearrange("p (c i j) -> p c j i", j=PACK, i=RUN),
            )
            return dealt

        def deal_fp4(name, raw):
            dealt = sbuf(name, [P, 2 * W], U8)
            nc.vector.tensor_copy(
                out=dealt[:].rearrange("p (j m b) -> p j m b", j=PACK, b=2),
                in_=raw.rearrange("p (m j b) -> p j m b", j=PACK, b=2),
            )
            return dealt

        wa0_scales = sbuf("wa0_scales", [P, W], U8)
        wa1_wc_scales = sbuf("wa1_wc_scales", [P, 2 * W], U8)
        wa0 = deal_fp8("wa0", wa_raw[:, 0, :])
        deal_scales(wa0_scales[:], plane(planes_first, 1), 1, 0, 1)
        deal_scales(wa0_scales[:], plane(planes_first, 1), 1, 1, PACK)
        wa1 = deal_fp8("wa1", wa_raw[:, 1, :])
        deal_scales(staged_dealt[:, 0:W], staged[:, 0:W], 1, 0, PACK)
        move_scales(planes_second, staged_dealt, 1, 0, 3)
        deal_scales(wa1_wc_scales[:], planes_rest[:, 2 * W : 4 * W], 2, 0, PACK)
        wc = deal_fp8("wc", wc_raw[:, 0, :])
        wb = deal_fp4("wb", wb_raw[:, 0, :])
        wy0 = deal_fp8("wy0", wy_raw[:, 0, :])
        wy1 = deal_fp8("wy1", wy_raw[:, 1, :])

        def token_matmul(acc, c, j, weight, weight_scales, tokens, token_scales, start, stop):
            nc.tensor.matmul_mx(
                out=acc[:, j, :],
                lhsT=weight[:, j * P : (j + 1) * P].bitcast(FP8X4),
                lhsT_scale=weight_scales[:, j * P : (j + 1) * P],
                rhs=tokens[:, 2 * c * CH : 2 * (c + 1) * CH].bitcast(FP4X4),
                rhs_scale=token_scales[:, c * CH : (c + 1) * CH],
                start=start,
                stop=stop,
            )

        def token_pass(acc, c, weight, weight_scales, tokens, token_scales, start, stop):
            for j in range(PACK):
                token_matmul(acc, c, j, weight, weight_scales, tokens, token_scales, start and j == 0, stop and j == PACK - 1)

        z_ps = [ps.tile([P, PACK, CH], F32, name="z%d" % c) for c in range(NCH)]
        for j in range(PACK):
            for c in range(NCH):
                token_matmul(z_ps[c], c, j, wa0, wa0_scales[:], xt[:, 0, :], xt0_plane, j == 0, False)
        for c in range(NCH):
            token_pass(z_ps[c], c, wa1, wa1_wc_scales[:, 0:W], xt[:, 1, :], xt1_plane, False, False)
            token_pass(z_ps[c], c, wc, wa1_wc_scales[:, W : 2 * W], xq[:, 0, :], xq_plane, False, True)
            lo = (c * CH + 1) * PACK
            nc.scalar.copy(
                out=z_sb[:, lo : lo + CH * PACK].rearrange("p (t j) -> p t j", j=PACK),
                in_=z_ps[c][:].rearrange("p j t -> p t j"),
            )

        def peak(c):
            hid = sbuf("hid%d" % c, [P, CH * PACK], BF16)
            lo = c * CH * PACK
            nc.vector.tensor_tensor(
                out=hid[:].rearrange("p (t j) -> p t j", j=PACK),
                in0=z_ps[c][:].rearrange("p j t -> p t j"),
                in1=z_sb[:, lo : lo + CH * PACK].rearrange("p (t j) -> p t j", j=PACK),
                op=mybir.AluOpType.max,
            )
            return hid

        def quantize_hid(c, hid):
            codes = sbuf("hid_codes%d" % c, [P, CH], I32)
            scales = sbuf("hid_scales%d" % c, [P, CH], U8)
            nc.vector.quantize_mx(out=codes[:].bitcast(FP8X4), scales=scales[:], in_=hid[:])
            return codes, scales

        y_codes = sbuf("y_codes", [P, T], I32)
        y_scales = sbuf("y_scales", [P, T], U8)
        out_rows = out_0.rearrange("(p j) t -> p j t", j=PACK)
        out_words = out_1[0].rearrange("p c t -> p (c t)").bitcast(I32)

        def second_layer(c, codes, scales):
            acc = ps.tile([P, PACK, CH], F32, name="y%d" % c)
            token_pass(acc, c, wy0, wy0_plane, xt[:, 0, :], xt0_plane, True, False)
            token_pass(acc, c, wy1, wy1_plane, xt[:, 1, :], xt1_plane, False, False)
            for j in range(PACK):
                nc.tensor.matmul_mx(
                    out=acc[:, j, :],
                    lhsT=wb[:, 2 * j * P : 2 * (j + 1) * P].bitcast(FP4X4),
                    lhsT_scale=wb_plane[:, j * P : (j + 1) * P],
                    rhs=codes[:].bitcast(FP8X4),
                    rhs_scale=scales[:],
                    start=False,
                    stop=j == PACK - 1,
                )
            y_sb = sbuf("y_sb%d" % c, [P, PACK, CH], F32)
            return acc, y_sb

        def copy_and_round(acc, y_sb, name, lo, hi):
            nc.scalar.copy(out=y_sb[:, :, lo:hi], in_=acc[:, :, lo:hi])
            rounded = sbuf(name, [P, (hi - lo) * PACK], BF16)
            nc.vector.tensor_copy(
                out=rounded[:].rearrange("p (u i j) -> p u j i", i=RUN, j=PACK),
                in_=y_sb[:, :, lo:hi].rearrange("p j (u i) -> p u j i", i=RUN),
            )
            return rounded

        def quantize_y(rounded, lo, hi):
            nc.vector.quantize_mx(out=y_codes[:, lo:hi].bitcast(FP8X4), scales=y_scales[:, lo:hi], in_=rounded[:])

        def store_y(c, y_sb):
            nc.sync.dma_start(out=out_rows[:, :, c * CH : (c + 1) * CH], in_=y_sb[:])

        def store_codes(lo, hi):
            nc.sync.dma_start(out=out_words[:, lo:hi], in_=y_codes[:, lo:hi])

        last = NCH - 1
        hid = [peak(0)]
        hid_mx = []
        for c in range(1, NCH):
            hid.append(peak(c))
            hid_mx.append(quantize_hid(c - 1, hid[c - 1]))

        rounded = []
        for c in range(last):
            acc, y_sb = second_layer(c, *hid_mx[c])
            rounded.append(copy_and_round(acc, y_sb, "y_bf%d" % c, 0, CH))
            store_y(c, y_sb)
            if c == 0:
                hid_mx.append(quantize_hid(last, hid[last]))
            else:
                quantize_y(rounded[c - 1], (c - 1) * CH, c * CH)
        store_codes(0, (last - 1) * CH)

        half = CH // 2
        acc, y_sb = second_layer(last, *hid_mx[last])
        first_half = copy_and_round(acc, y_sb, "y_bf_first_half", 0, half)
        quantize_y(rounded[last - 1], (last - 1) * CH, last * CH)
        second_half = copy_and_round(acc, y_sb, "y_bf_second_half", half, CH)
        store_y(last, y_sb)
        quantize_y(first_half, last * CH, last * CH + half)
        quantize_y(second_half, last * CH + half, T)
        store_codes((last - 1) * CH, T)
        for quad in range(4):
            queue = nc.sync if quad % 2 == 1 else nc.scalar
            queue.dma_start(
                out=out_2[0, 4 * quad : 4 * quad + 4, :].bitcast(I32),
                in_=y_scales[32 * quad : 32 * quad + 4, :].bitcast(I32),
            )
